import numpy as np
import ml_dtypes


def mxq(x, axis, fmt="e4m3"):
    dtype, down = {"e4m3": (ml_dtypes.float8_e4m3fn, 7), "e5m2": (ml_dtypes.float8_e5m2, 14)}[fmt]
    v = np.moveaxis(np.asarray(x, np.float32).astype(ml_dtypes.bfloat16).astype(np.float64), axis, -1)
    blocks = v.reshape(v.shape[:-1] + (-1, 32))
    amax = np.abs(blocks).max(-1, keepdims=True)
    byte = np.maximum(np.where(amax > 0, np.frexp(amax)[1] - 1 + 127, 0) - down, 1)
    scale = np.exp2(byte - 127.0)
    codes = (blocks / scale).astype(np.float32).astype(dtype).astype(np.float64)
    return np.moveaxis((codes * scale).reshape(v.shape), -1, axis)


WIDE = False


def mx_kscale(k):
    if not WIDE:
        return np.ones(k)
    levels = np.array([10, -10, 5, -5, 0])
    if k % 512:
        return np.exp2(np.random.permutation(np.resize(levels, k // 32))).repeat(32)
    a = np.empty((k // 512, 16))
    for p in range(k // 512):
        a[p, :8] = np.random.permutation(np.resize(levels, 8))
        for g in range(8):
            far = levels[np.abs(levels - a[p, g]) >= 10]
            a[p, g + 8] = far[np.random.randint(len(far))]
    return np.exp2(a.ravel()).repeat(32)


def f64(x):
    return np.asarray(x).astype(np.float64)


def striped(idx):
    return np.tile(idx.reshape(-1, 16).T, (8, 1)).astype(np.uint16)


def unstriped(offs):
    return offs[:16].T.reshape(-1).astype(np.int64)


E2M1 = np.array([0.0, 0.5, 1.0, 1.5, 2.0, 3.0, 4.0, 6.0, -0.0, -0.5, -1.0, -1.5, -2.0, -3.0, -4.0, -6.0])


def pack_weight(w, fmt):
    k, n = w.shape
    w = f64(np.asarray(w, np.float32).astype(ml_dtypes.bfloat16)).reshape(k // 32, 32, n)
    amax = np.abs(w).max(1)
    if fmt == "e4m3":
        byte = np.frexp(amax)[1] - 1 + 127 - 7
    else:
        mant, ex = np.frexp(amax / 6.0)
        byte = np.where(mant > 0.5, ex, ex - 1) + 127
    byte = np.clip(np.where(amax > 0, byte, 1), 1, 254)
    scaled = (w * np.exp2(127.0 - byte)[:, None, :]).reshape(k, n).astype(np.float32)
    by_word = np.ascontiguousarray(scaled.reshape(k // 512, 128, 4, n).transpose(0, 1, 3, 2))
    if fmt == "e4m3":
        words = by_word.astype(ml_dtypes.float8_e4m3fn).view(np.uint8)
    else:
        c = by_word.astype(ml_dtypes.float4_e2m1fn).view(np.uint8) & 0xF
        words = (c[..., 0::2] | (c[..., 1::2] << 4)).reshape(k // 512, 128, 2 * n)
    return np.ascontiguousarray(words), np.ascontiguousarray(byte.astype(np.uint8).reshape(k // 512, 16, n))


def unpack_weight(words, scales, fmt):
    g, _, n = scales.shape
    words = np.ascontiguousarray(words).reshape(g, 128, n, -1)
    if fmt == "e4m3":
        vals = words.view(ml_dtypes.float8_e4m3fn).astype(np.float64)
    else:
        nib = np.empty((g, 128, n, 4), np.uint8)
        nib[..., 0::2] = words & 0xF
        nib[..., 1::2] = words >> 4
        vals = E2M1[nib]
    vals = vals * np.repeat(np.exp2(scales.astype(np.float64) - 127.0), 8, axis=1)[..., None]
    return vals.transpose(0, 1, 3, 2).reshape(g * 512, n)


K, M, T, S = 1536, 512, 2048, 1024


def setup_inputs():
    n = np.random.standard_normal
    s = mx_kscale(K)[:, None]
    v = pack_weight(n((K, T)) * s, "e4m3")
    return {
        "tab_words": v[0],
        "tab_scales": v[1],
        "w": (n((K, M)) / np.sqrt(K) / s).astype(np.float32),
        "rT": n((M, T)).astype(np.float32),
        "b": (0.3 * n(512)).astype(np.float32),
        "offs": striped(np.random.permutation(T)[:S]),
    }


def reference(tab_words, tab_scales, w, rT, b, offs):
    tab_ = unpack_weight(tab_words, tab_scales, "e4m3")[:, unstriped(offs)]
    w_ = mxq(f64(w), 0, "e4m3")
    y = w_.T @ tab_
    return (y + f64(b)[:, None]) + f64(rT)[:, unstriped(offs)]

@@ -1,0 +1,122 @@
+from contextlib import ExitStack
+
+import concourse.mybir as mybir
+
+K, M, T, S = 1536, 512, 2048, 1024
+FLOPS = 2 * K * M * S
+
+F32 = mybir.dt.float32
+BF16 = mybir.dt.bfloat16
+I32 = mybir.dt.int32
+U32 = mybir.dt.uint32
+U16 = mybir.dt.uint16
+U8 = mybir.dt.uint8
+FP8X4 = mybir.dt.float8_e4m3fn_x4
+ADD = mybir.AluOpType.add
+IDENT = mybir.ActivationFunctionType.Identity
+
+P = 128
+PACK = 4
+PASSES = K // (P * PACK)
+ROW_TILES = M // P
+BANK = 512
+HALVES = S // BANK
+LIST_COLS = BANK // 16
+VEC_COLS = 256
+
+
+def tile_list_tabres_bias_kernel(tc, tab_words, tab_scales, w, rT, b, offs, out):
+    nc = tc.nc
+    with ExitStack() as ctx:
+        keep = ctx.enter_context(tc.tile_pool(name="keep", bufs=1))
+        psum = ctx.enter_context(tc.psum_pool(name="psum", bufs=1))
+
+        offsets = keep.tile([P, S // 16], U16, name="offsets")
+        nc.sync.dma_start(offsets[:], offs)
+
+        def picks(h):
+            return offsets[:, h * LIST_COLS : (h + 1) * LIST_COLS]
+
+        scale_window = keep.tile([P, T], U8, name="scale_window", align_bytes=64)
+        nc.gpsimd.memset(scale_window[:].bitcast(I32), 0)
+        for q in range(4):
+            nc.gpsimd.dma_start(
+                out=scale_window[32 * q : 32 * q + 4 * PASSES, :].bitcast(I32),
+                in_=tab_scales[:, 4 * q : 4 * q + 4, :].bitcast(I32),
+            )
+        bias = keep.tile([P, ROW_TILES], F32, name="bias")
+        with nc.allow_non_contiguous_dma("one bias value a partition"):
+            nc.scalar.dma_start(out=bias[:], in_=b.rearrange("(c p) -> p c", p=P))
+
+        w_raw = [keep.tile([P, PACK, M], F32, name="w_raw%d" % a) for a in range(PASSES)]
+        word_window = [keep.tile([P, T], U32, name="word_window%d" % a, align_bytes=64) for a in range(PASSES)]
+        res_window = [keep.tile([P, T], F32, name="res_window%d" % t, align_bytes=64) for t in range(ROW_TILES)]
+        for a in range(PASSES):
+            nc.sync.dma_start(
+                out=w_raw[a][:],
+                in_=w[a * P * PACK : (a + 1) * P * PACK, :].rearrange("(p j) n -> p j n", j=PACK),
+            )
+        for a in range(PASSES):
+            nc.sync.dma_start(
+                out=word_window[a][:].bitcast(I32),
+                in_=tab_words[a].rearrange("p t i -> p (t i)").bitcast(I32),
+            )
+        for t in range(ROW_TILES):
+            nc.sync.dma_start(out=res_window[t][:], in_=rT[t * P : (t + 1) * P, :])
+
+        picked_scales = keep.tile([P, S], U8, name="picked_scales", align_bytes=64)
+        nc.vector.tensor_copy(picked_scales[:], scale_window[:].indirect(offsets[:]))
+
+        w_codes, w_scales = [], []
+        for a in range(PASSES):
+            grouped = keep.tile([P, M, PACK], BF16, name="grouped%d" % a, align_bytes=64)
+            dst = grouped[:].rearrange("p (c i) j -> p c j i", i=4)
+            src = w_raw[a][:].rearrange("p j (c i) -> p c j i", i=4)
+            cut = VEC_COLS // 4
+            nc.vector.tensor_copy(out=dst[:, :cut], in_=src[:, :cut])
+            nc.scalar.copy(out=dst[:, cut:], in_=src[:, cut:])
+            codes = keep.tile([P, M], U32, name="w_codes%d" % a, align_bytes=64)
+            scales = keep.tile([P, M], U8, name="w_scales%d" % a, align_bytes=64)
+            nc.vector.quantize_mx(
+                out=codes[:].bitcast(FP8X4),
+                scales=scales[:],
+                in_=grouped[:].rearrange("p c j -> p (c j)"),
+            )
+            w_codes.append(codes)
+            w_scales.append(scales)
+
+        acc = {
+            (t, h): psum.tile([P, BANK], F32, name="acc%d_%d" % (t, h))
+            for t in range(ROW_TILES)
+            for h in range(HALVES)
+        }
+        for a in range(PASSES):
+            picked = []
+            for h in range(HALVES):
+                words = keep.tile([P, BANK], U32, name="picked%d_%d" % (a, h), align_bytes=64)
+                nc.vector.tensor_copy(words[:], word_window[a][:].indirect(picks(h)))
+                picked.append(words)
+            for t in range(ROW_TILES):
+                for h in range(HALVES):
+                    nc.tensor.matmul_mx(
+                        out=acc[t, h][:],
+                        lhsT=w_codes[a][:, t * P : (t + 1) * P].bitcast(FP8X4),
+                        lhsT_scale=w_scales[a][:, t * P : (t + 1) * P],
+                        rhs=picked[h][:].bitcast(FP8X4),
+                        rhs_scale=picked_scales[4 * a : P, h * BANK : (h + 1) * BANK],
+                        start=(a == 0),
+                        stop=(a == PASSES - 1),
+                    )
+
+        for t in range(ROW_TILES):
+            rows = slice(t * P, (t + 1) * P)
+            result = keep.tile([P, S], F32, name="result%d" % t)
+            for h in range(HALVES):
+                cols = slice(h * BANK, (h + 1) * BANK)
+                biased = keep.tile([P, BANK], F32, name="biased%d_%d" % (t, h))
+                nc.scalar.activation(out=biased[:], in_=acc[t, h][:], func=IDENT, bias=bias[:, t : t + 1])
+                nc.vector.tensor_tensor(result[:, cols], res_window[t][:].indirect(picks(h)), biased[:], ADD)
+                if t == ROW_TILES - 1:
+                    nc.sync.dma_start(out=out[rows, cols], in_=result[:, cols])
+            if t < ROW_TILES - 1:
+                nc.sync.dma_start(out=out[rows, :], in_=result[:])

@@ -1,6 +1,7 @@
 from contextlib import ExitStack
 
 import concourse.mybir as mybir
+from concourse.masks import make_identity
 
 K, M, T, S = 1536, 512, 2048, 1024
 FLOPS = 2 * K * M * S
@@ -21,7 +22,6 @@ PASSES = K // (P * PACK)
 ROW_TILES = M // P
 BANK = 512
 HALVES = S // BANK
-LIST_COLS = BANK // 16
 VEC_COLS = 256
 
 
@@ -34,36 +34,62 @@ def tile_list_tabres_bias_kernel(tc, tab_words, tab_scales, w, rT, b, offs, out)
         offsets = keep.tile([P, S // 16], U16, name="offsets")
         nc.sync.dma_start(offsets[:], offs)
 
-        def picks(h):
-            return offsets[:, h * LIST_COLS : (h + 1) * LIST_COLS]
+        def picks(cols):
+            return offsets[:, cols.start // 16 : cols.stop // 16]
+
+        whole = [slice(0, S)]
+        halves = [slice(h * BANK, (h + 1) * BANK) for h in range(HALVES)]
 
         scale_window = keep.tile([P, T], U8, name="scale_window", align_bytes=64)
         nc.gpsimd.memset(scale_window[:].bitcast(I32), 0)
-        for q in range(4):
-            nc.gpsimd.dma_start(
-                out=scale_window[32 * q : 32 * q + 4 * PASSES, :].bitcast(I32),
-                in_=tab_scales[:, 4 * q : 4 * q + 4, :].bitcast(I32),
-            )
-        bias = keep.tile([P, ROW_TILES], F32, name="bias")
-        with nc.allow_non_contiguous_dma("one bias value a partition"):
-            nc.scalar.dma_start(out=bias[:], in_=b.rearrange("(c p) -> p c", p=P))
+        bias_rows = keep.tile([P, P], F32, name="bias_rows")
+        nc.gpsimd.memset(bias_rows[:], 0.0)
+        nc.scalar.dma_start(out=bias_rows[0:ROW_TILES, :], in_=b.rearrange("(t p) -> t p", p=P))
+        identity = keep.tile([P, P], F32, name="identity")
+        make_identity(nc, identity[:])
 
         w_raw = [keep.tile([P, PACK, M], F32, name="w_raw%d" % a) for a in range(PASSES)]
         word_window = [keep.tile([P, T], U32, name="word_window%d" % a, align_bytes=64) for a in range(PASSES)]
         res_window = [keep.tile([P, T], F32, name="res_window%d" % t, align_bytes=64) for t in range(ROW_TILES)]
-        for a in range(PASSES):
-            nc.sync.dma_start(
-                out=w_raw[a][:],
-                in_=w[a * P * PACK : (a + 1) * P * PACK, :].rearrange("(p j) n -> p j n", j=PACK),
-            )
-        for a in range(PASSES):
+
+        def load_words(a):
             nc.sync.dma_start(
                 out=word_window[a][:].bitcast(I32),
                 in_=tab_words[a].rearrange("p t i -> p (t i)").bitcast(I32),
             )
+
+        def load_weight(a):
+            nc.sync.dma_start(
+                out=w_raw[a][:],
+                in_=w[a * P * PACK : (a + 1) * P * PACK, :].rearrange("(p j) n -> p j n", j=PACK),
+            )
+
+        load_words(0)
+        load_weight(0)
+        for q in range(4):
+            nc.sync.dma_start(
+                out=scale_window[32 * q : 32 * q + 4 * PASSES, :].bitcast(I32),
+                in_=tab_scales[:, 4 * q : 4 * q + 4, :].bitcast(I32),
+            )
+        for a in range(1, PASSES):
+            load_weight(a)
+        for a in range(1, PASSES):
+            load_words(a)
         for t in range(ROW_TILES):
             nc.sync.dma_start(out=res_window[t][:], in_=rT[t * P : (t + 1) * P, :])
 
+        turned = psum.tile([P, BANK], F32, name="turned", tag="bank0")
+        nc.tensor.transpose(turned[:, 0:P], bias_rows[:], identity[:])
+        bias = keep.tile([P, ROW_TILES], F32, name="bias")
+        nc.scalar.copy(out=bias[:], in_=turned[:, 0:ROW_TILES])
+
+        picked = [keep.tile([P, S], U32, name="picked%d" % a, align_bytes=64) for a in range(PASSES)]
+
+        def gather_words(a, pieces):
+            for cols in pieces:
+                nc.vector.tensor_copy(picked[a][:, cols], word_window[a][:].indirect(picks(cols)))
+
+        gather_words(0, whole)
         picked_scales = keep.tile([P, S], U8, name="picked_scales", align_bytes=64)
         nc.vector.tensor_copy(picked_scales[:], scale_window[:].indirect(offsets[:]))
 
@@ -72,8 +98,9 @@ def tile_list_tabres_bias_kernel(tc, tab_words, tab_scales, w, rT, b, offs, out)
             grouped = keep.tile([P, M, PACK], BF16, name="grouped%d" % a, align_bytes=64)
             dst = grouped[:].rearrange("p (c i) j -> p c j i", i=4)
             src = w_raw[a][:].rearrange("p j (c i) -> p c j i", i=4)
-            cut = VEC_COLS // 4
-            nc.vector.tensor_copy(out=dst[:, :cut], in_=src[:, :cut])
+            cut = 0 if a == 0 else VEC_COLS // 4
+            if cut:
+                nc.vector.tensor_copy(out=dst[:, :cut], in_=src[:, :cut])
             nc.scalar.copy(out=dst[:, cut:], in_=src[:, cut:])
             codes = keep.tile([P, M], U32, name="w_codes%d" % a, align_bytes=64)
             scales = keep.tile([P, M], U8, name="w_scales%d" % a, align_bytes=64)
@@ -86,37 +113,35 @@ def tile_list_tabres_bias_kernel(tc, tab_words, tab_scales, w, rT, b, offs, out)
             w_scales.append(scales)
 
         acc = {
-            (t, h): psum.tile([P, BANK], F32, name="acc%d_%d" % (t, h))
+            (t, h): psum.tile([P, BANK], F32, name="acc%d_%d" % (t, h), tag="bank%d" % (t * HALVES + h))
             for t in range(ROW_TILES)
             for h in range(HALVES)
         }
         for a in range(PASSES):
-            picked = []
-            for h in range(HALVES):
-                words = keep.tile([P, BANK], U32, name="picked%d_%d" % (a, h), align_bytes=64)
-                nc.vector.tensor_copy(words[:], word_window[a][:].indirect(picks(h)))
-                picked.append(words)
-            for t in range(ROW_TILES):
-                for h in range(HALVES):
-                    nc.tensor.matmul_mx(
-                        out=acc[t, h][:],
-                        lhsT=w_codes[a][:, t * P : (t + 1) * P].bitcast(FP8X4),
-                        lhsT_scale=w_scales[a][:, t * P : (t + 1) * P],
-                        rhs=picked[h][:].bitcast(FP8X4),
-                        rhs_scale=picked_scales[4 * a : P, h * BANK : (h + 1) * BANK],
-                        start=(a == 0),
-                        stop=(a == PASSES - 1),
-                    )
+            if a > 0:
+                gather_words(a, halves)
+            if a < PASSES - 1:
+                order = [(t, h) for h in range(HALVES) for t in range(ROW_TILES)]
+            else:
+                order = [(t, h) for t in range(ROW_TILES) for h in range(HALVES)]
+            for t, h in order:
+                nc.tensor.matmul_mx(
+                    out=acc[t, h][:],
+                    lhsT=w_codes[a][:, t * P : (t + 1) * P].bitcast(FP8X4),
+                    lhsT_scale=w_scales[a][:, t * P : (t + 1) * P],
+                    rhs=picked[a][:, halves[h]].bitcast(FP8X4),
+                    rhs_scale=picked_scales[4 * a : P, halves[h]],
+                    start=(a == 0),
+                    stop=(a == PASSES - 1),
+                )
 
         for t in range(ROW_TILES):
             rows = slice(t * P, (t + 1) * P)
+            biased = keep.tile([P, S], F32, name="biased%d" % t)
             result = keep.tile([P, S], F32, name="result%d" % t)
             for h in range(HALVES):
-                cols = slice(h * BANK, (h + 1) * BANK)
-                biased = keep.tile([P, BANK], F32, name="biased%d_%d" % (t, h))
-                nc.scalar.activation(out=biased[:], in_=acc[t, h][:], func=IDENT, bias=bias[:, t : t + 1])
-                nc.vector.tensor_tensor(result[:, cols], res_window[t][:].indirect(picks(h)), biased[:], ADD)
-                if t == ROW_TILES - 1:
-                    nc.sync.dma_start(out=out[rows, cols], in_=result[:, cols])
-            if t < ROW_TILES - 1:
-                nc.sync.dma_start(out=out[rows, :], in_=result[:])
+                nc.scalar.activation(out=biased[:, halves[h]], in_=acc[t, h][:], func=IDENT, bias=bias[:, t : t + 1])
+            for cols in halves if t in (0, ROW_TILES - 1) else whole:
+                nc.vector.tensor_tensor(result[:, cols], res_window[t][:].indirect(picks(cols)), biased[:, cols], ADD)
+            for cols in halves if t == ROW_TILES - 1 else whole:
+                nc.sync.dma_start(out=out[rows, cols], in_=result[:, cols])

@@ -14,7 +14,7 @@ U16 = mybir.dt.uint16
 U8 = mybir.dt.uint8
 FP8X4 = mybir.dt.float8_e4m3fn_x4
 ADD = mybir.AluOpType.add
-IDENT = mybir.ActivationFunctionType.Identity
+IDENTITY = mybir.ActivationFunctionType.Identity
 
 P = 128
 PACK = 4
@@ -22,7 +22,11 @@ PASSES = K // (P * PACK)
 ROW_TILES = M // P
 BANK = 512
 HALVES = S // BANK
-VEC_COLS = 256
+LIST_ROWS = 16
+QUADRANT = 32
+SCALE_ROWS = 4
+RUN = 4
+VECTOR_COLS = M // 2
 
 
 def tile_list_tabres_bias_kernel(tc, tab_words, tab_scales, w, rT, b, offs, out):
@@ -31,17 +35,18 @@ def tile_list_tabres_bias_kernel(tc, tab_words, tab_scales, w, rT, b, offs, out)
         keep = ctx.enter_context(tc.tile_pool(name="keep", bufs=1))
         psum = ctx.enter_context(tc.psum_pool(name="psum", bufs=1))
 
-        offsets = keep.tile([P, S // 16], U16, name="offsets")
-        nc.sync.dma_start(offsets[:], offs)
+        offsets = keep.tile([P, S // LIST_ROWS], U16, name="offsets")
 
         def picks(cols):
-            return offsets[:, cols.start // 16 : cols.stop // 16]
+            return offsets[:, cols.start // LIST_ROWS : cols.stop // LIST_ROWS]
 
         whole = [slice(0, S)]
         halves = [slice(h * BANK, (h + 1) * BANK) for h in range(HALVES)]
+        tapered = [slice(0, S // 2), slice(S // 2, 3 * S // 4), slice(3 * S // 4, S)]
 
         scale_window = keep.tile([P, T], U8, name="scale_window", align_bytes=64)
         nc.gpsimd.memset(scale_window[:].bitcast(I32), 0)
+
         bias_rows = keep.tile([P, P], F32, name="bias_rows")
         nc.gpsimd.memset(bias_rows[:], 0.0)
         nc.scalar.dma_start(out=bias_rows[0:ROW_TILES, :], in_=b.rearrange("(t p) -> t p", p=P))
@@ -65,15 +70,15 @@ def tile_list_tabres_bias_kernel(tc, tab_words, tab_scales, w, rT, b, offs, out)
             )
 
         load_words(0)
+        nc.sync.dma_start(offsets[:], offs)
         load_weight(0)
-        for q in range(4):
+        for q in range(P // QUADRANT):
             nc.sync.dma_start(
-                out=scale_window[32 * q : 32 * q + 4 * PASSES, :].bitcast(I32),
-                in_=tab_scales[:, 4 * q : 4 * q + 4, :].bitcast(I32),
+                out=scale_window[QUADRANT * q : QUADRANT * q + SCALE_ROWS * PASSES, :].bitcast(I32),
+                in_=tab_scales[:, SCALE_ROWS * q : SCALE_ROWS * (q + 1), :].bitcast(I32),
             )
         for a in range(1, PASSES):
             load_weight(a)
-        for a in range(1, PASSES):
             load_words(a)
         for t in range(ROW_TILES):
             nc.sync.dma_start(out=res_window[t][:], in_=rT[t * P : (t + 1) * P, :])
@@ -83,11 +88,11 @@ def tile_list_tabres_bias_kernel(tc, tab_words, tab_scales, w, rT, b, offs, out)
         bias = keep.tile([P, ROW_TILES], F32, name="bias")
         nc.scalar.copy(out=bias[:], in_=turned[:, 0:ROW_TILES])
 
-        picked = [keep.tile([P, S], U32, name="picked%d" % a, align_bytes=64) for a in range(PASSES)]
+        picked_words = [keep.tile([P, S], U32, name="picked_words%d" % a, align_bytes=64) for a in range(PASSES)]
 
         def gather_words(a, pieces):
             for cols in pieces:
-                nc.vector.tensor_copy(picked[a][:, cols], word_window[a][:].indirect(picks(cols)))
+                nc.vector.tensor_copy(picked_words[a][:, cols], word_window[a][:].indirect(picks(cols)))
 
         gather_words(0, whole)
         picked_scales = keep.tile([P, S], U8, name="picked_scales", align_bytes=64)
@@ -96,12 +101,12 @@ def tile_list_tabres_bias_kernel(tc, tab_words, tab_scales, w, rT, b, offs, out)
         w_codes, w_scales = [], []
         for a in range(PASSES):
             grouped = keep.tile([P, M, PACK], BF16, name="grouped%d" % a, align_bytes=64)
-            dst = grouped[:].rearrange("p (c i) j -> p c j i", i=4)
-            src = w_raw[a][:].rearrange("p j (c i) -> p c j i", i=4)
-            cut = 0 if a == 0 else VEC_COLS // 4
-            if cut:
-                nc.vector.tensor_copy(out=dst[:, :cut], in_=src[:, :cut])
-            nc.scalar.copy(out=dst[:, cut:], in_=src[:, cut:])
+            dst = grouped[:].rearrange("p (c i) j -> p c j i", i=RUN)
+            src = w_raw[a][:].rearrange("p j (c i) -> p c j i", i=RUN)
+            vector_runs = 0 if a == 0 else VECTOR_COLS // RUN
+            if vector_runs:
+                nc.vector.tensor_copy(out=dst[:, :vector_runs], in_=src[:, :vector_runs])
+            nc.scalar.copy(out=dst[:, vector_runs:], in_=src[:, vector_runs:])
             codes = keep.tile([P, M], U32, name="w_codes%d" % a, align_bytes=64)
             scales = keep.tile([P, M], U8, name="w_scales%d" % a, align_bytes=64)
             nc.vector.quantize_mx(
@@ -111,6 +116,8 @@ def tile_list_tabres_bias_kernel(tc, tab_words, tab_scales, w, rT, b, offs, out)
             )
             w_codes.append(codes)
             w_scales.append(scales)
+            if a > 0:
+                gather_words(a, whole if a < PASSES - 1 else halves)
 
         acc = {
             (t, h): psum.tile([P, BANK], F32, name="acc%d_%d" % (t, h), tag="bank%d" % (t * HALVES + h))
@@ -118,8 +125,6 @@ def tile_list_tabres_bias_kernel(tc, tab_words, tab_scales, w, rT, b, offs, out)
             for h in range(HALVES)
         }
         for a in range(PASSES):
-            if a > 0:
-                gather_words(a, halves)
             if a < PASSES - 1:
                 order = [(t, h) for h in range(HALVES) for t in range(ROW_TILES)]
             else:
@@ -129,19 +134,20 @@ def tile_list_tabres_bias_kernel(tc, tab_words, tab_scales, w, rT, b, offs, out)
                     out=acc[t, h][:],
                     lhsT=w_codes[a][:, t * P : (t + 1) * P].bitcast(FP8X4),
                     lhsT_scale=w_scales[a][:, t * P : (t + 1) * P],
-                    rhs=picked[a][:, halves[h]].bitcast(FP8X4),
-                    rhs_scale=picked_scales[4 * a : P, halves[h]],
+                    rhs=picked_words[a][:, halves[h]].bitcast(FP8X4),
+                    rhs_scale=picked_scales[SCALE_ROWS * a : P, halves[h]],
                     start=(a == 0),
                     stop=(a == PASSES - 1),
                 )
 
         for t in range(ROW_TILES):
             rows = slice(t * P, (t + 1) * P)
+            last = t == ROW_TILES - 1
             biased = keep.tile([P, S], F32, name="biased%d" % t)
             result = keep.tile([P, S], F32, name="result%d" % t)
             for h in range(HALVES):
-                nc.scalar.activation(out=biased[:, halves[h]], in_=acc[t, h][:], func=IDENT, bias=bias[:, t : t + 1])
-            for cols in halves if t in (0, ROW_TILES - 1) else whole:
+                nc.scalar.activation(out=biased[:, halves[h]], in_=acc[t, h][:], func=IDENTITY, bias=bias[:, t : t + 1])
+            for cols in tapered if last else halves if t == 0 else whole:
                 nc.vector.tensor_tensor(result[:, cols], res_window[t][:].indirect(picks(cols)), biased[:, cols], ADD)
-            for cols in halves if t == ROW_TILES - 1 else whole:
+            for cols in tapered if last else whole:
                 nc.sync.dma_start(out=out[rows, cols], in_=result[:, cols])

from contextlib import ExitStack

import concourse.mybir as mybir
from concourse.masks import make_identity

K, M, T, S = 1536, 512, 2048, 1024
FLOPS = 2 * K * M * S

F32 = mybir.dt.float32
BF16 = mybir.dt.bfloat16
I32 = mybir.dt.int32
U32 = mybir.dt.uint32
U16 = mybir.dt.uint16
U8 = mybir.dt.uint8
FP8X4 = mybir.dt.float8_e4m3fn_x4
ADD = mybir.AluOpType.add
IDENTITY = mybir.ActivationFunctionType.Identity

P = 128
PACK = 4
PASSES = K // (P * PACK)
ROW_TILES = M // P
BANK = 512
HALVES = S // BANK
LIST_ROWS = 16
QUADRANT = 32
SCALE_ROWS = 4
RUN = 4
VECTOR_COLS = M // 2


def tile_list_tabres_bias_kernel(tc, tab_words, tab_scales, w, rT, b, offs, out):
    nc = tc.nc
    with ExitStack() as ctx:
        keep = ctx.enter_context(tc.tile_pool(name="keep", bufs=1))
        psum = ctx.enter_context(tc.psum_pool(name="psum", bufs=1))

        offsets = keep.tile([P, S // LIST_ROWS], U16, name="offsets")

        def picks(cols):
            return offsets[:, cols.start // LIST_ROWS : cols.stop // LIST_ROWS]

        whole = [slice(0, S)]
        halves = [slice(h * BANK, (h + 1) * BANK) for h in range(HALVES)]
        tapered = [slice(0, S // 2), slice(S // 2, 3 * S // 4), slice(3 * S // 4, S)]

        scale_window = keep.tile([P, T], U8, name="scale_window", align_bytes=64)
        nc.gpsimd.memset(scale_window[:].bitcast(I32), 0)

        bias_rows = keep.tile([P, P], F32, name="bias_rows")
        nc.gpsimd.memset(bias_rows[:], 0.0)
        nc.scalar.dma_start(out=bias_rows[0:ROW_TILES, :], in_=b.rearrange("(t p) -> t p", p=P))
        identity = keep.tile([P, P], F32, name="identity")
        make_identity(nc, identity[:])

        w_raw = [keep.tile([P, PACK, M], F32, name="w_raw%d" % a) for a in range(PASSES)]
        word_window = [keep.tile([P, T], U32, name="word_window%d" % a, align_bytes=64) for a in range(PASSES)]
        res_window = [keep.tile([P, T], F32, name="res_window%d" % t, align_bytes=64) for t in range(ROW_TILES)]

        def load_words(a):
            nc.sync.dma_start(
                out=word_window[a][:].bitcast(I32),
                in_=tab_words[a].rearrange("p t i -> p (t i)").bitcast(I32),
            )

        def load_weight(a):
            nc.sync.dma_start(
                out=w_raw[a][:],
                in_=w[a * P * PACK : (a + 1) * P * PACK, :].rearrange("(p j) n -> p j n", j=PACK),
            )

        load_words(0)
        nc.sync.dma_start(offsets[:], offs)
        load_weight(0)
        for q in range(P // QUADRANT):
            nc.sync.dma_start(
                out=scale_window[QUADRANT * q : QUADRANT * q + SCALE_ROWS * PASSES, :].bitcast(I32),
                in_=tab_scales[:, SCALE_ROWS * q : SCALE_ROWS * (q + 1), :].bitcast(I32),
            )
        for a in range(1, PASSES):
            load_weight(a)
            load_words(a)
        for t in range(ROW_TILES):
            nc.sync.dma_start(out=res_window[t][:], in_=rT[t * P : (t + 1) * P, :])

        turned = psum.tile([P, BANK], F32, name="turned", tag="bank0")
        nc.tensor.transpose(turned[:, 0:P], bias_rows[:], identity[:])
        bias = keep.tile([P, ROW_TILES], F32, name="bias")
        nc.scalar.copy(out=bias[:], in_=turned[:, 0:ROW_TILES])

        picked_words = [keep.tile([P, S], U32, name="picked_words%d" % a, align_bytes=64) for a in range(PASSES)]

        def gather_words(a, pieces):
            for cols in pieces:
                nc.vector.tensor_copy(picked_words[a][:, cols], word_window[a][:].indirect(picks(cols)))

        gather_words(0, whole)
        picked_scales = keep.tile([P, S], U8, name="picked_scales", align_bytes=64)
        nc.vector.tensor_copy(picked_scales[:], scale_window[:].indirect(offsets[:]))

        w_codes, w_scales = [], []
        for a in range(PASSES):
            grouped = keep.tile([P, M, PACK], BF16, name="grouped%d" % a, align_bytes=64)
            dst = grouped[:].rearrange("p (c i) j -> p c j i", i=RUN)
            src = w_raw[a][:].rearrange("p j (c i) -> p c j i", i=RUN)
            vector_runs = 0 if a == 0 else VECTOR_COLS // RUN
            if vector_runs:
                nc.vector.tensor_copy(out=dst[:, :vector_runs], in_=src[:, :vector_runs])
            nc.scalar.copy(out=dst[:, vector_runs:], in_=src[:, vector_runs:])
            codes = keep.tile([P, M], U32, name="w_codes%d" % a, align_bytes=64)
            scales = keep.tile([P, M], U8, name="w_scales%d" % a, align_bytes=64)
            nc.vector.quantize_mx(
                out=codes[:].bitcast(FP8X4),
                scales=scales[:],
                in_=grouped[:].rearrange("p c j -> p (c j)"),
            )
            w_codes.append(codes)
            w_scales.append(scales)
            if a > 0:
                gather_words(a, whole if a < PASSES - 1 else halves)

        acc = {
            (t, h): psum.tile([P, BANK], F32, name="acc%d_%d" % (t, h), tag="bank%d" % (t * HALVES + h))
            for t in range(ROW_TILES)
            for h in range(HALVES)
        }
        for a in range(PASSES):
            if a < PASSES - 1:
                order = [(t, h) for h in range(HALVES) for t in range(ROW_TILES)]
            else:
                order = [(t, h) for t in range(ROW_TILES) for h in range(HALVES)]
            for t, h in order:
                nc.tensor.matmul_mx(
                    out=acc[t, h][:],
                    lhsT=w_codes[a][:, t * P : (t + 1) * P].bitcast(FP8X4),
                    lhsT_scale=w_scales[a][:, t * P : (t + 1) * P],
                    rhs=picked_words[a][:, halves[h]].bitcast(FP8X4),
                    rhs_scale=picked_scales[SCALE_ROWS * a : P, halves[h]],
                    start=(a == 0),
                    stop=(a == PASSES - 1),
                )

        for t in range(ROW_TILES):
            rows = slice(t * P, (t + 1) * P)
            last = t == ROW_TILES - 1
            biased = keep.tile([P, S], F32, name="biased%d" % t)
            result = keep.tile([P, S], F32, name="result%d" % t)
            for h in range(HALVES):
                nc.scalar.activation(out=biased[:, halves[h]], in_=acc[t, h][:], func=IDENTITY, bias=bias[:, t : t + 1])
            for cols in tapered if last else halves if t == 0 else whole:
                nc.vector.tensor_tensor(result[:, cols], res_window[t][:].indirect(picks(cols)), biased[:, cols], ADD)
            for cols in tapered if last else whole:
                nc.sync.dma_start(out=out[rows, cols], in_=result[:, cols])
